import numpy as np
import ml_dtypes


def mxq(x, axis, fmt="e4m3"):
    dtype, down = {"e4m3": (ml_dtypes.float8_e4m3fn, 7), "e5m2": (ml_dtypes.float8_e5m2, 14)}[fmt]
    v = np.moveaxis(np.asarray(x, np.float32).astype(ml_dtypes.bfloat16).astype(np.float64), axis, -1)
    blocks = v.reshape(v.shape[:-1] + (-1, 32))
    amax = np.abs(blocks).max(-1, keepdims=True)
    byte = np.maximum(np.where(amax > 0, np.frexp(amax)[1] - 1 + 127, 0) - down, 1)
    scale = np.exp2(byte - 127.0)
    codes = (blocks / scale).astype(np.float32).astype(dtype).astype(np.float64)
    return np.moveaxis((codes * scale).reshape(v.shape), -1, axis)


WIDE = False


def mx_kscale(k):
    if not WIDE:
        return np.ones(k)
    levels = np.array([10, -10, 5, -5, 0])
    if k % 512:
        return np.exp2(np.random.permutation(np.resize(levels, k // 32))).repeat(32)
    a = np.empty((k // 512, 16))
    for p in range(k // 512):
        a[p, :8] = np.random.permutation(np.resize(levels, 8))
        for g in range(8):
            far = levels[np.abs(levels - a[p, g]) >= 10]
            a[p, g + 8] = far[np.random.randint(len(far))]
    return np.exp2(a.ravel()).repeat(32)


def f64(x):
    return np.asarray(x).astype(np.float64)


def striped(idx):
    return np.tile(np.asarray(idx).reshape(-1, 16).T, (8, 1)).astype(np.uint16)


def unstriped(offs):
    return offs[:16].T.reshape(-1).astype(np.int64)


E2M1 = np.array([0.0, 0.5, 1.0, 1.5, 2.0, 3.0, 4.0, 6.0, -0.0, -0.5, -1.0, -1.5, -2.0, -3.0, -4.0, -6.0])


def pack_weight(w, fmt):
    k, n = w.shape
    w = f64(np.asarray(w, np.float32).astype(ml_dtypes.bfloat16)).reshape(k // 32, 32, n)
    amax = np.abs(w).max(1)
    if fmt == "e4m3":
        byte = np.frexp(amax)[1] - 1 + 127 - 7
    else:
        mant, ex = np.frexp(amax / 6.0)
        byte = np.where(mant > 0.5, ex, ex - 1) + 127
    byte = np.clip(np.where(amax > 0, byte, 1), 1, 254)
    scaled = (w * np.exp2(127.0 - byte)[:, None, :]).reshape(k, n).astype(np.float32)
    by_word = np.ascontiguousarray(scaled.reshape(k // 512, 128, 4, n).transpose(0, 1, 3, 2))
    if fmt == "e4m3":
        words = by_word.astype(ml_dtypes.float8_e4m3fn).view(np.uint8)
    else:
        c = by_word.astype(ml_dtypes.float4_e2m1fn).view(np.uint8) & 0xF
        words = (c[..., 0::2] | (c[..., 1::2] << 4)).reshape(k // 512, 128, 2 * n)
    return np.ascontiguousarray(words), np.ascontiguousarray(byte.astype(np.uint8).reshape(k // 512, 16, n))


def unpack_weight(words, scales, fmt):
    g, _, n = scales.shape
    words = np.ascontiguousarray(words).reshape(g, 128, n, -1)
    if fmt == "e4m3":
        vals = words.view(ml_dtypes.float8_e4m3fn).astype(np.float64)
    else:
        nib = np.empty((g, 128, n, 4), np.uint8)
        nib[..., 0::2] = words & 0xF
        nib[..., 1::2] = words >> 4
        vals = E2M1[nib]
    vals = vals * np.repeat(np.exp2(scales.astype(np.float64) - 127.0), 8, axis=1)[..., None]
    return vals.transpose(0, 1, 3, 2).reshape(g * 512, n)


B, N, T, D, NQ = 1, 512, 2048, 512, 256


def setup_inputs():
    n = np.random.standard_normal
    idx = np.random.permutation(T)[:B * N]
    s = mx_kscale(D)[:, None]
    mid = n((D, T))
    kp = pack_weight((mid + np.abs(n((D, T)))) / s, "e4m3")
    cp = pack_weight((mid - np.abs(n((D, T)))) / s, "e4m3")
    return {
        "qT": (n((B, D, NQ)) * s * (1.00 / np.sqrt(D))).astype(np.float32),
        "k_words": kp[0],
        "k_scales": kp[1],
        "c_words": cp[0],
        "c_scales": cp[1],
        "th": (14 + n((B, NQ, 1))).astype(np.float32),
        "offs": striped(idx),
    }


def reference(qT, k_words, k_scales, c_words, c_scales, th, offs):
    idx = unstriped(offs)
    pick = lambda x, which: x[:, which].reshape(x.shape[0], B, -1).transpose(1, 0, 2)
    k = unpack_weight(k_words, k_scales, "e4m3")
    kg = pick(k, idx)
    c = unpack_weight(c_words, c_scales, "e4m3")
    cg = pick(c, idx)
    hiq = mxq(np.maximum(f64(qT), 0.0), 1, "e4m3")
    loq = mxq(np.minimum(f64(qT), 0.0), 1, "e4m3")
    a = (hiq.transpose(0, 2, 1) @ kg) + (loq.transpose(0, 2, 1) @ cg)
    y = np.maximum(a - f64(th), 0.0)
    return y

@@ -1,0 +1,118 @@
+from contextlib import ExitStack
+
+import concourse.mybir as mybir
+
+D, T, N, NQ = 512, 2048, 512, 256
+FLOPS = 2 * 2 * NQ * D * N
+
+F32 = mybir.dt.float32
+BF16 = mybir.dt.bfloat16
+I32 = mybir.dt.int32
+U32 = mybir.dt.uint32
+U16 = mybir.dt.uint16
+U8 = mybir.dt.uint8
+FP8X4 = mybir.dt.float8_e4m3fn_x4
+ALU = mybir.AluOpType
+ACT = mybir.ActivationFunctionType
+
+P = 128
+PACK = 4
+HALF = N // 2
+C_ROW = 4
+
+
+def tile_attend_questthr_topk_kernel(tc, qT, k_words, k_scales, c_words, c_scales, th, offs, out):
+    nc = tc.nc
+    with ExitStack() as ctx:
+        pool = ctx.enter_context(tc.tile_pool(name="held", bufs=1))
+        psum = ctx.enter_context(tc.psum_pool(name="psum", bufs=1))
+
+        offsets = pool.tile([P, N // 16], U16, name="offsets")
+        q_raw = pool.tile([P, PACK, NQ], F32, name="q_raw", tag="q", align_bytes=64)
+        k_pool = pool.tile([P, T], I32, name="k_pool", tag="k", align_bytes=64)
+        ks_pool = pool.tile([P, T], U8, name="ks_pool", tag="ks", align_bytes=64)
+        cs_pool = pool.tile([P, T], U8, name="cs_pool", tag="cs", align_bytes=64)
+        th_col = pool.tile([P, 2], F32, name="th_col", tag="c", align_bytes=64)
+        th_neg = pool.tile([P, 2], F32, name="th_neg")
+
+        nc.vector.memset(ks_pool[:].bitcast(I32), 0)
+        nc.vector.memset(cs_pool[:].bitcast(I32), 0)
+
+        nc.sync.dma_start(offsets[:], offs)
+        with nc.allow_non_contiguous_dma(reason="one threshold a partition"):
+            nc.sync.dma_start(out=th_col[:], in_=th[0].rearrange("(t p) o -> p (t o)", p=P))
+        nc.scalar.dma_start(out=q_raw[:], in_=qT[0].rearrange("(p j) w -> p j w", j=PACK))
+        for quad in range(4):
+            nc.sync.dma_start(
+                out=ks_pool[32 * quad : 32 * quad + 4, :].bitcast(I32),
+                in_=k_scales[0, 4 * quad : 4 * quad + 4, :].bitcast(I32),
+            )
+        nc.scalar.dma_start(out=k_pool[:], in_=k_words[0].rearrange("p n t -> p (n t)").bitcast(I32))
+        for quad in range(4):
+            (nc.sync if quad < 2 else nc.gpsimd).dma_start(
+                out=cs_pool[32 * quad + C_ROW : 32 * quad + C_ROW + 4, :].bitcast(I32),
+                in_=c_scales[0, 4 * quad : 4 * quad + 4, :].bitcast(I32),
+            )
+
+        nc.scalar.activation(out=th_neg[:], in_=th_col[:], func=ACT.Copy, scale=-1.0)
+        c_pool = pool.tile([P, T], I32, name="c_pool", tag="c", align_bytes=64)
+        nc.scalar.dma_start(out=c_pool[:], in_=c_words[0].rearrange("p n t -> p (n t)").bitcast(I32))
+
+        q_by_word = q_raw[:].rearrange("p j w -> p w j")
+        hi = pool.tile([P, NQ, PACK], BF16, name="hi", tag="hi", align_bytes=64)
+        nc.scalar.activation(out=hi[:], in_=q_by_word, func=ACT.Relu)
+
+        ks = pool.tile([P, N], U8, name="ks", tag="ks_out", align_bytes=64)
+        nc.vector.tensor_copy(ks[:], ks_pool[:].indirect(offsets[:]))
+        lo = pool.tile([P, NQ, PACK], BF16, name="lo", align_bytes=64)
+        nc.vector.tensor_scalar_min(lo[:], q_by_word, 0.0)
+        hi_codes = pool.tile([P, NQ], U32, name="hi_codes", tag="ks", align_bytes=64)
+        lo_codes = pool.tile([P, NQ], U32, name="lo_codes", align_bytes=64)
+        hi_scales = pool.tile([P, NQ], U8, name="hi_scales", align_bytes=64)
+        lo_scales = pool.tile([P, NQ], U8, name="lo_scales", align_bytes=64)
+        nc.vector.quantize_mx(out=hi_codes[:].bitcast(FP8X4), scales=hi_scales[:], in_=hi[:].rearrange("p w j -> p (w j)"))
+        nc.vector.quantize_mx(out=lo_codes[:].bitcast(FP8X4), scales=lo_scales[:], in_=lo[:].rearrange("p w j -> p (w j)"))
+        cs = pool.tile([P, N], U8, name="cs", tag="cs_out", align_bytes=64)
+        nc.vector.tensor_copy(cs[:], cs_pool[:].indirect(offsets[:]))
+        kw = pool.tile([P, N], U32, name="kw", tag="hi", align_bytes=64)
+        nc.vector.tensor_copy(kw[:], k_pool[:].bitcast(U32).indirect(offsets[:]))
+        cw = pool.tile([P, N], U32, name="cw", tag="cs", align_bytes=64)
+        for h in range(2):
+            nc.vector.tensor_copy(
+                cw[:, h * HALF : (h + 1) * HALF],
+                c_pool[:].bitcast(U32).indirect(offsets[:, 16 * h : 16 * (h + 1)]),
+            )
+
+        acc = {(h, t): psum.tile([P, HALF], F32, name=f"acc{h}{t}") for h in range(2) for t in range(2)}
+        for h in range(2):
+            slots = slice(h * HALF, (h + 1) * HALF)
+            for t in range(2):
+                rows = slice(t * P, (t + 1) * P)
+                nc.tensor.matmul_mx(
+                    out=acc[h, t][:],
+                    lhsT=hi_codes[:, rows].bitcast(FP8X4),
+                    lhsT_scale=hi_scales[:, rows],
+                    rhs=kw[:, slots].bitcast(FP8X4),
+                    rhs_scale=ks[:, slots],
+                    start=True,
+                    stop=False,
+                )
+        for h in range(2):
+            slots = slice(h * HALF, (h + 1) * HALF)
+            for t in range(2):
+                rows = slice(t * P, (t + 1) * P)
+                nc.tensor.matmul_mx(
+                    out=acc[h, t][:],
+                    lhsT=lo_codes[:, rows].bitcast(FP8X4),
+                    lhsT_scale=lo_scales[:, rows],
+                    rhs=cw[:, slots].bitcast(FP8X4),
+                    rhs_scale=cs[C_ROW:P, slots],
+                    start=False,
+                    stop=True,
+                )
+                res = pool.tile([P, HALF], F32, name=f"res{h}{t}")
+                if t == 0:
+                    nc.scalar.activation(out=res[:], in_=acc[h, t][:], func=ACT.Relu, bias=th_neg[:, 0:1])
+                else:
+                    nc.vector.tensor_scalar(res[:], acc[h, t][:], th_neg[:, 1:2], 0.0, ALU.add, ALU.max)
+                nc.sync.dma_start(out=out[0, rows, slots], in_=res[:])

@@ -28,60 +28,58 @@ def tile_attend_questthr_topk_kernel(tc, qT, k_words, k_scales, c_words, c_scale
         psum = ctx.enter_context(tc.psum_pool(name="psum", bufs=1))
 
         offsets = pool.tile([P, N // 16], U16, name="offsets")
-        q_raw = pool.tile([P, PACK, NQ], F32, name="q_raw", tag="q", align_bytes=64)
-        k_pool = pool.tile([P, T], I32, name="k_pool", tag="k", align_bytes=64)
-        ks_pool = pool.tile([P, T], U8, name="ks_pool", tag="ks", align_bytes=64)
-        cs_pool = pool.tile([P, T], U8, name="cs_pool", tag="cs", align_bytes=64)
-        th_col = pool.tile([P, 2], F32, name="th_col", tag="c", align_bytes=64)
         th_neg = pool.tile([P, 2], F32, name="th_neg")
+        th_a = pool.tile([P, 1], F32, name="th_a", tag="k", align_bytes=64)
+        th_b = pool.tile([P, 1], F32, name="th_b", tag="cs", align_bytes=64)
+        q_raw = pool.tile([P, PACK, NQ], F32, name="q_raw", tag="c", align_bytes=64)
+        ks_pool = pool.tile([P, T], U8, name="ks_pool", align_bytes=64)
+
+        def load_scale_rows(plane, scales, first_row):
+            for quad in range(4):
+                nc.sync.dma_start(
+                    out=plane[32 * quad + first_row : 32 * quad + first_row + 4, :].bitcast(I32),
+                    in_=scales[0, 4 * quad : 4 * quad + 4, :].bitcast(I32),
+                )
 
         nc.vector.memset(ks_pool[:].bitcast(I32), 0)
-        nc.vector.memset(cs_pool[:].bitcast(I32), 0)
-
+        nc.sync.dma_start(out=th_a[:], in_=th[0, 0:P, :])
+        nc.sync.dma_start(out=th_b[:], in_=th[0, P : 2 * P, :])
         nc.sync.dma_start(offsets[:], offs)
-        with nc.allow_non_contiguous_dma(reason="one threshold a partition"):
-            nc.sync.dma_start(out=th_col[:], in_=th[0].rearrange("(t p) o -> p (t o)", p=P))
-        nc.scalar.dma_start(out=q_raw[:], in_=qT[0].rearrange("(p j) w -> p j w", j=PACK))
-        for quad in range(4):
-            nc.sync.dma_start(
-                out=ks_pool[32 * quad : 32 * quad + 4, :].bitcast(I32),
-                in_=k_scales[0, 4 * quad : 4 * quad + 4, :].bitcast(I32),
-            )
-        nc.scalar.dma_start(out=k_pool[:], in_=k_words[0].rearrange("p n t -> p (n t)").bitcast(I32))
-        for quad in range(4):
-            (nc.sync if quad < 2 else nc.gpsimd).dma_start(
-                out=cs_pool[32 * quad + C_ROW : 32 * quad + C_ROW + 4, :].bitcast(I32),
-                in_=c_scales[0, 4 * quad : 4 * quad + 4, :].bitcast(I32),
-            )
+        nc.sync.dma_start(out=q_raw[:], in_=qT[0].rearrange("(p j) w -> p j w", j=PACK))
+        load_scale_rows(ks_pool, k_scales, 0)
 
-        nc.scalar.activation(out=th_neg[:], in_=th_col[:], func=ACT.Copy, scale=-1.0)
-        c_pool = pool.tile([P, T], I32, name="c_pool", tag="c", align_bytes=64)
-        nc.scalar.dma_start(out=c_pool[:], in_=c_words[0].rearrange("p n t -> p (n t)").bitcast(I32))
+        nc.vector.tensor_scalar_mul(th_neg[:, 0:1], th_a[:], -1.0)
+        nc.vector.tensor_scalar_mul(th_neg[:, 1:2], th_b[:], -1.0)
+        k_pool = pool.tile([P, T], I32, name="k_pool", tag="k", align_bytes=64)
+        nc.sync.dma_start(out=k_pool[:], in_=k_words[0].rearrange("p n t -> p (n t)").bitcast(I32))
+        cs_pool = pool.tile([P, T], U8, name="cs_pool", tag="cs", align_bytes=64)
+        nc.vector.memset(cs_pool[:].bitcast(I32), 0)
+        load_scale_rows(cs_pool, c_scales, C_ROW)
 
-        q_by_word = q_raw[:].rearrange("p j w -> p w j")
-        hi = pool.tile([P, NQ, PACK], BF16, name="hi", tag="hi", align_bytes=64)
-        nc.scalar.activation(out=hi[:], in_=q_by_word, func=ACT.Relu)
-
-        ks = pool.tile([P, N], U8, name="ks", tag="ks_out", align_bytes=64)
-        nc.vector.tensor_copy(ks[:], ks_pool[:].indirect(offsets[:]))
+        ks = pool.tile([P, N], U8, name="ks", align_bytes=64)
+        cs = pool.tile([P, N], U8, name="cs", tag="cs_out", align_bytes=64)
+        kw = pool.tile([P, N], U32, name="kw", align_bytes=64)
+        cw = [pool.tile([P, HALF], U32, name=f"cw{h}", align_bytes=64) for h in range(2)]
+        hi = pool.tile([P, NQ, PACK], BF16, name="hi", align_bytes=64)
         lo = pool.tile([P, NQ, PACK], BF16, name="lo", align_bytes=64)
-        nc.vector.tensor_scalar_min(lo[:], q_by_word, 0.0)
-        hi_codes = pool.tile([P, NQ], U32, name="hi_codes", tag="ks", align_bytes=64)
+        hi_codes = pool.tile([P, NQ], U32, name="hi_codes", align_bytes=64)
         lo_codes = pool.tile([P, NQ], U32, name="lo_codes", align_bytes=64)
         hi_scales = pool.tile([P, NQ], U8, name="hi_scales", align_bytes=64)
         lo_scales = pool.tile([P, NQ], U8, name="lo_scales", align_bytes=64)
+
+        q_by_word = q_raw[:].rearrange("p j w -> p w j")
+        nc.scalar.activation(out=hi[:], in_=q_by_word, func=ACT.Relu)
+        nc.vector.tensor_scalar_min(lo[:], q_by_word, 0.0)
+        c_pool = pool.tile([P, T], I32, name="c_pool", tag="c", align_bytes=64)
+        nc.sync.dma_start(out=c_pool[:], in_=c_words[0].rearrange("p n t -> p (n t)").bitcast(I32))
+
+        nc.vector.tensor_copy(ks[:], ks_pool[:].indirect(offsets[:]))
         nc.vector.quantize_mx(out=hi_codes[:].bitcast(FP8X4), scales=hi_scales[:], in_=hi[:].rearrange("p w j -> p (w j)"))
         nc.vector.quantize_mx(out=lo_codes[:].bitcast(FP8X4), scales=lo_scales[:], in_=lo[:].rearrange("p w j -> p (w j)"))
-        cs = pool.tile([P, N], U8, name="cs", tag="cs_out", align_bytes=64)
-        nc.vector.tensor_copy(cs[:], cs_pool[:].indirect(offsets[:]))
-        kw = pool.tile([P, N], U32, name="kw", tag="hi", align_bytes=64)
         nc.vector.tensor_copy(kw[:], k_pool[:].bitcast(U32).indirect(offsets[:]))
-        cw = pool.tile([P, N], U32, name="cw", tag="cs", align_bytes=64)
+        nc.vector.tensor_copy(cs[:], cs_pool[:].indirect(offsets[:]))
         for h in range(2):
-            nc.vector.tensor_copy(
-                cw[:, h * HALF : (h + 1) * HALF],
-                c_pool[:].bitcast(U32).indirect(offsets[:, 16 * h : 16 * (h + 1)]),
-            )
+            nc.vector.tensor_copy(cw[h][:], c_pool[:].bitcast(U32).indirect(offsets[:, 16 * h : 16 * (h + 1)]))
 
         acc = {(h, t): psum.tile([P, HALF], F32, name=f"acc{h}{t}") for h in range(2) for t in range(2)}
         for h in range(2):
@@ -105,7 +103,7 @@ def tile_attend_questthr_topk_kernel(tc, qT, k_words, k_scales, c_words, c_scale
                     out=acc[h, t][:],
                     lhsT=lo_codes[:, rows].bitcast(FP8X4),
                     lhsT_scale=lo_scales[:, rows],
-                    rhs=cw[:, slots].bitcast(FP8X4),
+                    rhs=cw[h][:].bitcast(FP8X4),
                     rhs_scale=cs[C_ROW:P, slots],
                     start=False,
                     stop=True,

@@ -29,10 +29,11 @@ def tile_attend_questthr_topk_kernel(tc, qT, k_words, k_scales, c_words, c_scale
 
         offsets = pool.tile([P, N // 16], U16, name="offsets")
         th_neg = pool.tile([P, 2], F32, name="th_neg")
-        th_a = pool.tile([P, 1], F32, name="th_a", tag="k", align_bytes=64)
-        th_b = pool.tile([P, 1], F32, name="th_b", tag="cs", align_bytes=64)
-        q_raw = pool.tile([P, PACK, NQ], F32, name="q_raw", tag="c", align_bytes=64)
-        ks_pool = pool.tile([P, T], U8, name="ks_pool", align_bytes=64)
+        th_col = pool.tile([P, 2], F32, name="th_col", tag="c", align_bytes=64)
+        q_raw = pool.tile([P, PACK, NQ], F32, name="q_raw")
+        k_pool = pool.tile([P, T], I32, name="k_pool", align_bytes=64)
+        cs_pool = pool.tile([P, T], U8, name="cs_pool", align_bytes=64)
+        ks_pool = pool.tile([P, T], U8, name="ks_pool", tag="ks", align_bytes=64)
 
         def load_scale_rows(plane, scales, first_row):
             for quad in range(4):
@@ -42,23 +43,18 @@ def tile_attend_questthr_topk_kernel(tc, qT, k_words, k_scales, c_words, c_scale
                 )
 
         nc.vector.memset(ks_pool[:].bitcast(I32), 0)
-        nc.sync.dma_start(out=th_a[:], in_=th[0, 0:P, :])
-        nc.sync.dma_start(out=th_b[:], in_=th[0, P : 2 * P, :])
+        nc.vector.memset(cs_pool[:].bitcast(I32), 0)
+        nc.gpsimd.dma_start(out=k_pool[:], in_=k_words[0].rearrange("p n t -> p (n t)").bitcast(I32))
+        with nc.allow_non_contiguous_dma(reason="one threshold a partition"):
+            nc.sync.dma_start(out=th_col[:], in_=th[0].rearrange("(t p) o -> p (t o)", p=P))
         nc.sync.dma_start(offsets[:], offs)
         nc.sync.dma_start(out=q_raw[:], in_=qT[0].rearrange("(p j) w -> p j w", j=PACK))
         load_scale_rows(ks_pool, k_scales, 0)
-
-        nc.vector.tensor_scalar_mul(th_neg[:, 0:1], th_a[:], -1.0)
-        nc.vector.tensor_scalar_mul(th_neg[:, 1:2], th_b[:], -1.0)
-        k_pool = pool.tile([P, T], I32, name="k_pool", tag="k", align_bytes=64)
-        nc.sync.dma_start(out=k_pool[:], in_=k_words[0].rearrange("p n t -> p (n t)").bitcast(I32))
-        cs_pool = pool.tile([P, T], U8, name="cs_pool", tag="cs", align_bytes=64)
-        nc.vector.memset(cs_pool[:].bitcast(I32), 0)
         load_scale_rows(cs_pool, c_scales, C_ROW)
+        nc.vector.tensor_scalar_mul(th_neg[:], th_col[:], -1.0)
 
-        ks = pool.tile([P, N], U8, name="ks", align_bytes=64)
-        cs = pool.tile([P, N], U8, name="cs", tag="cs_out", align_bytes=64)
-        kw = pool.tile([P, N], U32, name="kw", align_bytes=64)
+        ks = pool.tile([P, N], U8, name="ks", tag="ks_out", align_bytes=64)
+        cs = pool.tile([P, N], U8, name="cs", align_bytes=64)
         cw = [pool.tile([P, HALF], U32, name=f"cw{h}", align_bytes=64) for h in range(2)]
         hi = pool.tile([P, NQ, PACK], BF16, name="hi", align_bytes=64)
         lo = pool.tile([P, NQ, PACK], BF16, name="lo", align_bytes=64)
@@ -76,6 +72,7 @@ def tile_attend_questthr_topk_kernel(tc, qT, k_words, k_scales, c_words, c_scale
         nc.vector.tensor_copy(ks[:], ks_pool[:].indirect(offsets[:]))
         nc.vector.quantize_mx(out=hi_codes[:].bitcast(FP8X4), scales=hi_scales[:], in_=hi[:].rearrange("p w j -> p (w j)"))
         nc.vector.quantize_mx(out=lo_codes[:].bitcast(FP8X4), scales=lo_scales[:], in_=lo[:].rearrange("p w j -> p (w j)"))
+        kw = pool.tile([P, N], U32, name="kw", tag="ks", align_bytes=64)
         nc.vector.tensor_copy(kw[:], k_pool[:].bitcast(U32).indirect(offsets[:]))
         nc.vector.tensor_copy(cs[:], cs_pool[:].indirect(offsets[:]))
         for h in range(2):

@@ -36,10 +36,10 @@ def tile_attend_questthr_topk_kernel(tc, qT, k_words, k_scales, c_words, c_scale
         ks_pool = pool.tile([P, T], U8, name="ks_pool", tag="ks", align_bytes=64)
 
         def load_scale_rows(plane, scales, first_row):
-            for quad in range(4):
+            for r in range(4):
                 nc.sync.dma_start(
-                    out=plane[32 * quad + first_row : 32 * quad + first_row + 4, :].bitcast(I32),
-                    in_=scales[0, 4 * quad : 4 * quad + 4, :].bitcast(I32),
+                    out=plane[first_row + r : P : 32, :].bitcast(I32),
+                    in_=scales[0, r:16:4, :].bitcast(I32),
                 )
 
         nc.vector.memset(ks_pool[:].bitcast(I32), 0)

@@ -63,9 +63,9 @@ def tile_attend_questthr_topk_kernel(tc, qT, k_words, k_scales, c_words, c_scale
         hi_scales = pool.tile([P, NQ], U8, name="hi_scales", align_bytes=64)
         lo_scales = pool.tile([P, NQ], U8, name="lo_scales", align_bytes=64)
 
-        q_by_word = q_raw[:].rearrange("p j w -> p w j")
-        nc.scalar.activation(out=hi[:], in_=q_by_word, func=ACT.Relu)
-        nc.vector.tensor_scalar_min(lo[:], q_by_word, 0.0)
+        q_by_word = q_raw[:].rearrange("p j (c i) -> p c j i", i=4)
+        nc.scalar.activation(out=hi[:].rearrange("p (c i) j -> p c j i", i=4), in_=q_by_word, func=ACT.Relu)
+        nc.vector.tensor_scalar_min(lo[:].rearrange("p (c i) j -> p c j i", i=4), q_by_word, 0.0)
         c_pool = pool.tile([P, T], I32, name="c_pool", tag="c", align_bytes=64)
         nc.sync.dma_start(out=c_pool[:], in_=c_words[0].rearrange("p n t -> p (n t)").bitcast(I32))
 

from contextlib import ExitStack

import concourse.mybir as mybir

D, T, N, NQ = 512, 2048, 512, 256
FLOPS = 2 * 2 * NQ * D * N

F32 = mybir.dt.float32
BF16 = mybir.dt.bfloat16
I32 = mybir.dt.int32
U32 = mybir.dt.uint32
U16 = mybir.dt.uint16
U8 = mybir.dt.uint8
FP8X4 = mybir.dt.float8_e4m3fn_x4
ALU = mybir.AluOpType
ACT = mybir.ActivationFunctionType

P = 128
PACK = 4
HALF = N // 2
C_ROW = 4


def tile_attend_questthr_topk_kernel(tc, qT, k_words, k_scales, c_words, c_scales, th, offs, out):
    nc = tc.nc
    with ExitStack() as ctx:
        pool = ctx.enter_context(tc.tile_pool(name="held", bufs=1))
        psum = ctx.enter_context(tc.psum_pool(name="psum", bufs=1))

        offsets = pool.tile([P, N // 16], U16, name="offsets")
        th_neg = pool.tile([P, 2], F32, name="th_neg")
        th_col = pool.tile([P, 2], F32, name="th_col", tag="c", align_bytes=64)
        q_raw = pool.tile([P, PACK, NQ], F32, name="q_raw")
        k_pool = pool.tile([P, T], I32, name="k_pool", align_bytes=64)
        cs_pool = pool.tile([P, T], U8, name="cs_pool", align_bytes=64)
        ks_pool = pool.tile([P, T], U8, name="ks_pool", tag="ks", align_bytes=64)

        def load_scale_rows(plane, scales, first_row):
            for r in range(4):
                nc.sync.dma_start(
                    out=plane[first_row + r : P : 32, :].bitcast(I32),
                    in_=scales[0, r:16:4, :].bitcast(I32),
                )

        nc.vector.memset(ks_pool[:].bitcast(I32), 0)
        nc.vector.memset(cs_pool[:].bitcast(I32), 0)
        nc.gpsimd.dma_start(out=k_pool[:], in_=k_words[0].rearrange("p n t -> p (n t)").bitcast(I32))
        with nc.allow_non_contiguous_dma(reason="one threshold a partition"):
            nc.sync.dma_start(out=th_col[:], in_=th[0].rearrange("(t p) o -> p (t o)", p=P))
        nc.sync.dma_start(offsets[:], offs)
        nc.sync.dma_start(out=q_raw[:], in_=qT[0].rearrange("(p j) w -> p j w", j=PACK))
        load_scale_rows(ks_pool, k_scales, 0)
        load_scale_rows(cs_pool, c_scales, C_ROW)
        nc.vector.tensor_scalar_mul(th_neg[:], th_col[:], -1.0)

        ks = pool.tile([P, N], U8, name="ks", tag="ks_out", align_bytes=64)
        cs = pool.tile([P, N], U8, name="cs", align_bytes=64)
        cw = [pool.tile([P, HALF], U32, name=f"cw{h}", align_bytes=64) for h in range(2)]
        hi = pool.tile([P, NQ, PACK], BF16, name="hi", align_bytes=64)
        lo = pool.tile([P, NQ, PACK], BF16, name="lo", align_bytes=64)
        hi_codes = pool.tile([P, NQ], U32, name="hi_codes", align_bytes=64)
        lo_codes = pool.tile([P, NQ], U32, name="lo_codes", align_bytes=64)
        hi_scales = pool.tile([P, NQ], U8, name="hi_scales", align_bytes=64)
        lo_scales = pool.tile([P, NQ], U8, name="lo_scales", align_bytes=64)

        q_by_word = q_raw[:].rearrange("p j (c i) -> p c j i", i=4)
        nc.scalar.activation(out=hi[:].rearrange("p (c i) j -> p c j i", i=4), in_=q_by_word, func=ACT.Relu)
        nc.vector.tensor_scalar_min(lo[:].rearrange("p (c i) j -> p c j i", i=4), q_by_word, 0.0)
        c_pool = pool.tile([P, T], I32, name="c_pool", tag="c", align_bytes=64)
        nc.sync.dma_start(out=c_pool[:], in_=c_words[0].rearrange("p n t -> p (n t)").bitcast(I32))

        nc.vector.tensor_copy(ks[:], ks_pool[:].indirect(offsets[:]))
        nc.vector.quantize_mx(out=hi_codes[:].bitcast(FP8X4), scales=hi_scales[:], in_=hi[:].rearrange("p w j -> p (w j)"))
        nc.vector.quantize_mx(out=lo_codes[:].bitcast(FP8X4), scales=lo_scales[:], in_=lo[:].rearrange("p w j -> p (w j)"))
        kw = pool.tile([P, N], U32, name="kw", tag="ks", align_bytes=64)
        nc.vector.tensor_copy(kw[:], k_pool[:].bitcast(U32).indirect(offsets[:]))
        nc.vector.tensor_copy(cs[:], cs_pool[:].indirect(offsets[:]))
        for h in range(2):
            nc.vector.tensor_copy(cw[h][:], c_pool[:].bitcast(U32).indirect(offsets[:, 16 * h : 16 * (h + 1)]))

        acc = {(h, t): psum.tile([P, HALF], F32, name=f"acc{h}{t}") for h in range(2) for t in range(2)}
        for h in range(2):
            slots = slice(h * HALF, (h + 1) * HALF)
            for t in range(2):
                rows = slice(t * P, (t + 1) * P)
                nc.tensor.matmul_mx(
                    out=acc[h, t][:],
                    lhsT=hi_codes[:, rows].bitcast(FP8X4),
                    lhsT_scale=hi_scales[:, rows],
                    rhs=kw[:, slots].bitcast(FP8X4),
                    rhs_scale=ks[:, slots],
                    start=True,
                    stop=False,
                )
        for h in range(2):
            slots = slice(h * HALF, (h + 1) * HALF)
            for t in range(2):
                rows = slice(t * P, (t + 1) * P)
                nc.tensor.matmul_mx(
                    out=acc[h, t][:],
                    lhsT=lo_codes[:, rows].bitcast(FP8X4),
                    lhsT_scale=lo_scales[:, rows],
                    rhs=cw[h][:].bitcast(FP8X4),
                    rhs_scale=cs[C_ROW:P, slots],
                    start=False,
                    stop=True,
                )
                res = pool.tile([P, HALF], F32, name=f"res{h}{t}")
                if t == 0:
                    nc.scalar.activation(out=res[:], in_=acc[h, t][:], func=ACT.Relu, bias=th_neg[:, 0:1])
                else:
                    nc.vector.tensor_scalar(res[:], acc[h, t][:], th_neg[:, 1:2], 0.0, ALU.add, ALU.max)
                nc.sync.dma_start(out=out[0, rows, slots], in_=res[:])
